import numpy as np
CORES = [1,129,9,137,17,145,25,153,33,161,41,169,49,177,57,185,65,193,73,201,81,209,89,217,97,225,105,233,113,241,121,249]
N = 32
def setup_inputs(rng):
    return {"x1": rng.standard_normal((N, 128, 32), dtype=np.float32), "x2": rng.standard_normal((N, 128, 64), dtype=np.float32)}
def reference(x1, x2):
    out = []
    s = x1.sum(axis=0, dtype=np.float64).astype(x1.dtype)
    b = 32 // N
    out.append(np.stack([s[:, r * b:(r + 1) * b] for r in range(N)]))
    g = np.concatenate(list(x2), axis=1)
    out.append(np.broadcast_to(g, (N,) + g.shape))
    return {"y1": out[0], "y2": out[1]}

@@ -1,0 +1,130 @@
+from concourse.bass import DstId, RemoteDMATransfer
+from concourse.mybir import AluOpType
+
+SCRATCH = {
+    "img": ("sbuf", [128, 2048], "float32"),
+    "x1s": ("sbuf", [128, 32], "float32"),
+    "rs": ("sbuf", [128, 32], "float32"),
+    "par": ("sbuf", [128, 2], "float32"),
+}
+SEMAPHORES = [
+    "ld1", "ld2",
+    "own",
+    "arr",
+    "rarr",
+    "parr",
+    "snt",
+    "acc",
+    "st1", "st2",
+]
+
+RANK = 1
+COLLECTOR = 3
+LANES = {2: (0, 1), 3: (2, 3), 6: (4, 5), 7: (6, 7)}
+DIE1_OFFSETS = (0, 1, 2, 3)
+OFF_CHIP, ON_CHIP = 0x00FF, 0xFF00
+
+
+def rank_program(g, core, T, topo):
+    h, chip, k = topo.host(core), topo.chip(core), core % 8
+    if k != RANK and k not in LANES:
+        return
+    q, m = chip % 2, chip // 2
+    S = T.sem
+
+    def at(hh, mm, qq, kk):
+        return hh * 128 + (2 * (mm % 8) + qq) * 8 + kk
+
+    def to(dst):
+        rid, pid = topo.addr(dst, core)
+        return DstId(rid=rid, pnc=pid)
+
+    def block(hh, mm, qq):
+        c = 64 * (4 * (mm % 8) + 2 * qq + hh)
+        return T.img[:, c:c + 64]
+
+    def pair(mm, qq):
+        c = 64 * (4 * (mm % 8) + 2 * qq)
+        return T.img[:, c:c + 128]
+
+    def copy(ap, dsts, mask, sem):
+        return RemoteDMATransfer(dst_ids=[to(d) for d in dsts], dma_engine_mask=mask, remote_sem=sem,
+                                 srcs=[ap], dsts=[ap for d in dsts])
+
+    mine = block(h, m, q)
+
+    if k == RANK:
+        g.sync.dma_start(mine, T.x2[:]).then_inc(S.ld2, 16)
+        g.scalar.dma_start(T.x1s[:], T.x1[:]).then_inc(S.ld1, 16)
+
+        lane_of = {o: kk for kk in LANES for o in LANES[kk]}
+        plane7 = [at(hh, m - o, q, lane_of[o]) for o in DIE1_OFFSETS for hh in (0, 1) if (o, hh) != (0, h)]
+        g.wait_ge(S.ld2, 16)
+        g.remote_dma_fused([copy(mine, [at(h, m, q, kk) for kk in (2, 6, 7)], ON_CHIP, S.own),
+                            copy(mine, plane7, OFF_CHIP, S.arr)], local_sem=S.snt)
+        sent = 16
+
+        me = 2 * m + h
+        slot = T.rs[:, 2 * me:2 * me + 2]
+        trs = []
+        for step in range(1, 17):
+            i = (me + step) % 16
+            mm, hh = i // 2, i % 2
+            c0 = 4 * mm + 2 * hh
+            mask = ON_CHIP if i == me else 1 << ((step - 1) % 8)
+            trs.append(RemoteDMATransfer(dst_ids=[to(at(hh, mm, q, COLLECTOR))], dma_engine_mask=mask,
+                                         remote_sem=S.rarr, srcs=[T.x1s[:, c0:c0 + 2]], dsts=[slot]))
+        g.wait_ge(S.ld1, 16)
+        g.remote_dma_fused(trs[0:8], local_sem=S.snt)
+        g.remote_dma_fused(trs[8:16], local_sem=S.snt)
+        sent += 15 + 8
+
+        g.sync.wait_ge(S.ld2, 16)
+        g.sync.wait_ge(S.arr, 64)
+        g.sync.dma_start(T.y2[:], T.img[:]).then_inc(S.st2, 16)
+
+        g.wait_ge(S.parr, 8)
+        g.dma_start(T.par[:, 0:1], T.par[:, 1:2], accum_op=AluOpType.add).then_inc(S.acc, 16)
+        g.wait_ge(S.acc, 16)
+        g.scalar.wait_ge(S.acc, 16)
+        g.scalar.dma_start(T.y1[:], T.par[:, 0:1]).then_inc(S.st1, 16)
+
+        g.wait_ge(S.snt, sent)
+        g.wait_ge(S.st1, 16)
+        g.wait_ge(S.st2, 16)
+        return
+
+    sent = 0
+    o0, o1 = LANES[k]
+
+    if k == COLLECTOR:
+        g.wait_ge(S.rarr, 15 + 8)
+        g.remote_dma_fused([
+            RemoteDMATransfer(dst_ids=[to(at(j, m, h, RANK))], dma_engine_mask=0x0F << (4 * j), remote_sem=S.parr,
+                              srcs=[T.rs[:, 2 * i + j:2 * i + j + 1] for i in range(16)], dsts=[T.par[:, q:q + 1]],
+                              alu_op=1)
+            for j in (0, 1)], local_sem=S.snt)
+        sent += 8
+
+    if o0 not in DIE1_OFFSETS:
+        g.wait_ge(S.own, 8)
+        g.remote_dma_fused([copy(mine, [at(hh, m - o, q, k) for o in (o0, o1) for hh in (0, 1)], OFF_CHIP, S.arr)],
+                           local_sem=S.snt)
+        sent += 8
+
+    here, mate = at(h, m, q, RANK), at(h, m, 1 - q, RANK)
+    if o0 == 0:
+        g.wait_ge(S.own, 8)
+        g.wait_ge(S.arr, 3 * 8)
+    else:
+        g.wait_ge(S.arr, 4 * 8)
+    trs = [copy(pair(m + o0, q), [mate], 0x000F, S.arr),
+           copy(pair(m + o1, q), [mate], 0x00F0, S.arr),
+           copy(pair(m + o1, q), [here], 0xF000, S.arr)]
+    if o0 != 0:
+        trs.append(copy(pair(m + o0, q), [here], 0x0F00, S.arr))
+    g.remote_dma_fused(trs, local_sem=S.snt)
+    if o0 == 0:
+        g.remote_dma_fused([copy(block(1 - h, m, q), [here], 0x0F00, S.arr)], local_sem=S.snt)
+    sent += 16
+    g.wait_ge(S.snt, sent)

@@ -1,28 +1,26 @@
 from concourse.bass import DstId, RemoteDMATransfer
-from concourse.mybir import AluOpType
 
 SCRATCH = {
     "img": ("sbuf", [128, 2048], "float32"),
-    "x1s": ("sbuf", [128, 32], "float32"),
-    "rs": ("sbuf", [128, 32], "float32"),
-    "par": ("sbuf", [128, 2], "float32"),
+    "xd": ("dram", [16 * 128, 2], "float32"),
+    "cd": ("dram", [17 * 128, 2], "float32"),
+    "sd": ("dram", [16 * 128, 2], "float32"),
 }
 SEMAPHORES = [
     "ld1", "ld2",
     "own",
     "arr",
     "rarr",
-    "parr",
+    "msum",
+    "sarr",
     "snt",
-    "acc",
     "st1", "st2",
 ]
 
 RANK = 1
 COLLECTOR = 3
 LANES = {2: (0, 1), 3: (2, 3), 6: (4, 5), 7: (6, 7)}
-DIE1_OFFSETS = (0, 1, 2, 3)
-OFF_CHIP, ON_CHIP = 0x00FF, 0xFF00
+OFF_CHIP = 0x00FF
 
 
 def rank_program(g, core, T, topo):
@@ -30,6 +28,7 @@ def rank_program(g, core, T, topo):
     if k != RANK and k not in LANES:
         return
     q, m = chip % 2, chip // 2
+    me = 2 * m + h
     S = T.sem
 
     def at(hh, mm, qq, kk):
@@ -51,73 +50,57 @@ def rank_program(g, core, T, topo):
         return RemoteDMATransfer(dst_ids=[to(d) for d in dsts], dma_engine_mask=mask, remote_sem=sem,
                                  srcs=[ap], dsts=[ap for d in dsts])
 
+    def slab(t, i):
+        return t[128 * i:128 * (i + 1), :]
+
     mine = block(h, m, q)
 
     if k == RANK:
+        r = T.rank_of(core)
         g.sync.dma_start(mine, T.x2[:]).then_inc(S.ld2, 16)
-        g.scalar.dma_start(T.x1s[:], T.x1[:]).then_inc(S.ld1, 16)
+        g.scalar.dma_start(T.xd[:], T.x1[:]).then_inc(S.ld1, 16)
 
-        lane_of = {o: kk for kk in LANES for o in LANES[kk]}
-        plane7 = [at(hh, m - o, q, lane_of[o]) for o in DIE1_OFFSETS for hh in (0, 1) if (o, hh) != (0, h)]
         g.wait_ge(S.ld2, 16)
-        g.remote_dma_fused([copy(mine, [at(h, m, q, kk) for kk in (2, 6, 7)], ON_CHIP, S.own),
-                            copy(mine, plane7, OFF_CHIP, S.arr)], local_sem=S.snt)
-        sent = 16
+        g.remote_dma_fused([copy(mine, [at(h, m, q, kk) for kk in LANES], 0xFFFF, S.own)], local_sem=S.snt)
 
-        me = 2 * m + h
-        slot = T.rs[:, 2 * me:2 * me + 2]
         trs = []
         for step in range(1, 17):
             i = (me + step) % 16
-            mm, hh = i // 2, i % 2
-            c0 = 4 * mm + 2 * hh
-            mask = ON_CHIP if i == me else 1 << ((step - 1) % 8)
-            trs.append(RemoteDMATransfer(dst_ids=[to(at(hh, mm, q, COLLECTOR))], dma_engine_mask=mask,
-                                         remote_sem=S.rarr, srcs=[T.x1s[:, c0:c0 + 2]], dsts=[slot]))
+            trs.append(RemoteDMATransfer(dst_ids=[to(at(i % 2, i // 2, q, COLLECTOR))],
+                                         dma_engine_mask=1 << (8 if i == me else (step - 1) % 8),
+                                         remote_sem=S.rarr, srcs=[slab(T.xd, i)], dsts=[slab(T.cd, me)]))
         g.wait_ge(S.ld1, 16)
         g.remote_dma_fused(trs[0:8], local_sem=S.snt)
         g.remote_dma_fused(trs[8:16], local_sem=S.snt)
-        sent += 15 + 8
 
         g.sync.wait_ge(S.ld2, 16)
         g.sync.wait_ge(S.arr, 64)
         g.sync.dma_start(T.y2[:], T.img[:]).then_inc(S.st2, 16)
 
-        g.wait_ge(S.parr, 8)
-        g.dma_start(T.par[:, 0:1], T.par[:, 1:2], accum_op=AluOpType.add).then_inc(S.acc, 16)
-        g.wait_ge(S.acc, 16)
-        g.scalar.wait_ge(S.acc, 16)
-        g.scalar.dma_start(T.y1[:], T.par[:, 0:1]).then_inc(S.st1, 16)
+        g.wait_ge(S.sarr, 16 * 8)
+        g.dma_start(T.y1[:], T.sd[r // 2::16, r % 2:r % 2 + 1], allow_slow_non_contiguous=True).then_inc(S.st1, 16)
 
-        g.wait_ge(S.snt, sent)
+        g.wait_ge(S.snt, 16 + 16)
         g.wait_ge(S.st1, 16)
         g.wait_ge(S.st2, 16)
         return
 
-    sent = 0
     o0, o1 = LANES[k]
 
-    if k == COLLECTOR:
-        g.wait_ge(S.rarr, 15 + 8)
-        g.remote_dma_fused([
-            RemoteDMATransfer(dst_ids=[to(at(j, m, h, RANK))], dma_engine_mask=0x0F << (4 * j), remote_sem=S.parr,
-                              srcs=[T.rs[:, 2 * i + j:2 * i + j + 1] for i in range(16)], dsts=[T.par[:, q:q + 1]],
-                              alu_op=1)
-            for j in (0, 1)], local_sem=S.snt)
-        sent += 8
+    plane = [at(hh, m - o, q, k) for o in (o0, o1) for hh in (0, 1) if (o, hh) != (0, h)]
+    g.wait_ge(S.own, 16)
+    g.remote_dma_fused([copy(mine, plane, OFF_CHIP, S.arr)], local_sem=S.snt)
+    sent = 8
 
-    if o0 not in DIE1_OFFSETS:
-        g.wait_ge(S.own, 8)
-        g.remote_dma_fused([copy(mine, [at(hh, m - o, q, k) for o in (o0, o1) for hh in (0, 1)], OFF_CHIP, S.arr)],
-                           local_sem=S.snt)
+    if k == COLLECTOR:
+        g.wait_ge(S.rarr, 16)
+        g.remote_dma_fused([RemoteDMATransfer(dst_ids=[to(at(h, m, 1 - q, COLLECTOR))], dma_engine_mask=OFF_CHIP,
+                                              remote_sem=S.msum, srcs=[slab(T.cd, i) for i in range(16)],
+                                              dsts=[slab(T.cd, 16)], alu_op=1)], local_sem=S.snt)
         sent += 8
 
     here, mate = at(h, m, q, RANK), at(h, m, 1 - q, RANK)
-    if o0 == 0:
-        g.wait_ge(S.own, 8)
-        g.wait_ge(S.arr, 3 * 8)
-    else:
-        g.wait_ge(S.arr, 4 * 8)
+    g.wait_ge(S.arr, 8 * len(plane))
     trs = [copy(pair(m + o0, q), [mate], 0x000F, S.arr),
            copy(pair(m + o1, q), [mate], 0x00F0, S.arr),
            copy(pair(m + o1, q), [here], 0xF000, S.arr)]
@@ -127,4 +110,13 @@ def rank_program(g, core, T, topo):
     if o0 == 0:
         g.remote_dma_fused([copy(block(1 - h, m, q), [here], 0x0F00, S.arr)], local_sem=S.snt)
     sent += 16
+
+    if k == COLLECTOR:
+        g.wait_ge(S.msum, 8)
+        g.remote_dma_fused([RemoteDMATransfer(dst_ids=[to(at(i % 2, i // 2, q, RANK)) for i in range(16)],
+                                              dma_engine_mask=OFF_CHIP, remote_sem=S.sarr,
+                                              srcs=[slab(T.cd, i) for i in range(17)],
+                                              dsts=[slab(T.sd, me) for i in range(16)], alu_op=1)], local_sem=S.snt)
+        sent += 8
+
     g.wait_ge(S.snt, sent)

from concourse.bass import DstId, RemoteDMATransfer

SCRATCH = {
    "img": ("sbuf", [128, 2048], "float32"),
    "xd": ("dram", [16 * 128, 2], "float32"),
    "cd": ("dram", [17 * 128, 2], "float32"),
    "sd": ("dram", [16 * 128, 2], "float32"),
}
SEMAPHORES = [
    "ld1", "ld2",
    "own",
    "arr",
    "rarr",
    "msum",
    "sarr",
    "snt",
    "st1", "st2",
]

RANK = 1
COLLECTOR = 3
LANES = {2: (0, 1), 3: (2, 3), 6: (4, 5), 7: (6, 7)}
OFF_CHIP = 0x00FF


def rank_program(g, core, T, topo):
    h, chip, k = topo.host(core), topo.chip(core), core % 8
    if k != RANK and k not in LANES:
        return
    q, m = chip % 2, chip // 2
    me = 2 * m + h
    S = T.sem

    def at(hh, mm, qq, kk):
        return hh * 128 + (2 * (mm % 8) + qq) * 8 + kk

    def to(dst):
        rid, pid = topo.addr(dst, core)
        return DstId(rid=rid, pnc=pid)

    def block(hh, mm, qq):
        c = 64 * (4 * (mm % 8) + 2 * qq + hh)
        return T.img[:, c:c + 64]

    def pair(mm, qq):
        c = 64 * (4 * (mm % 8) + 2 * qq)
        return T.img[:, c:c + 128]

    def copy(ap, dsts, mask, sem):
        return RemoteDMATransfer(dst_ids=[to(d) for d in dsts], dma_engine_mask=mask, remote_sem=sem,
                                 srcs=[ap], dsts=[ap for d in dsts])

    def slab(t, i):
        return t[128 * i:128 * (i + 1), :]

    mine = block(h, m, q)

    if k == RANK:
        r = T.rank_of(core)
        g.sync.dma_start(mine, T.x2[:]).then_inc(S.ld2, 16)
        g.scalar.dma_start(T.xd[:], T.x1[:]).then_inc(S.ld1, 16)

        g.wait_ge(S.ld2, 16)
        g.remote_dma_fused([copy(mine, [at(h, m, q, kk) for kk in LANES], 0xFFFF, S.own)], local_sem=S.snt)

        trs = []
        for step in range(1, 17):
            i = (me + step) % 16
            trs.append(RemoteDMATransfer(dst_ids=[to(at(i % 2, i // 2, q, COLLECTOR))],
                                         dma_engine_mask=1 << (8 if i == me else (step - 1) % 8),
                                         remote_sem=S.rarr, srcs=[slab(T.xd, i)], dsts=[slab(T.cd, me)]))
        g.wait_ge(S.ld1, 16)
        g.remote_dma_fused(trs[0:8], local_sem=S.snt)
        g.remote_dma_fused(trs[8:16], local_sem=S.snt)

        g.sync.wait_ge(S.ld2, 16)
        g.sync.wait_ge(S.arr, 64)
        g.sync.dma_start(T.y2[:], T.img[:]).then_inc(S.st2, 16)

        g.wait_ge(S.sarr, 16 * 8)
        g.dma_start(T.y1[:], T.sd[r // 2::16, r % 2:r % 2 + 1], allow_slow_non_contiguous=True).then_inc(S.st1, 16)

        g.wait_ge(S.snt, 16 + 16)
        g.wait_ge(S.st1, 16)
        g.wait_ge(S.st2, 16)
        return

    o0, o1 = LANES[k]

    plane = [at(hh, m - o, q, k) for o in (o0, o1) for hh in (0, 1) if (o, hh) != (0, h)]
    g.wait_ge(S.own, 16)
    g.remote_dma_fused([copy(mine, plane, OFF_CHIP, S.arr)], local_sem=S.snt)
    sent = 8

    if k == COLLECTOR:
        g.wait_ge(S.rarr, 16)
        g.remote_dma_fused([RemoteDMATransfer(dst_ids=[to(at(h, m, 1 - q, COLLECTOR))], dma_engine_mask=OFF_CHIP,
                                              remote_sem=S.msum, srcs=[slab(T.cd, i) for i in range(16)],
                                              dsts=[slab(T.cd, 16)], alu_op=1)], local_sem=S.snt)
        sent += 8

    here, mate = at(h, m, q, RANK), at(h, m, 1 - q, RANK)
    g.wait_ge(S.arr, 8 * len(plane))
    trs = [copy(pair(m + o0, q), [mate], 0x000F, S.arr),
           copy(pair(m + o1, q), [mate], 0x00F0, S.arr),
           copy(pair(m + o1, q), [here], 0xF000, S.arr)]
    if o0 != 0:
        trs.append(copy(pair(m + o0, q), [here], 0x0F00, S.arr))
    g.remote_dma_fused(trs, local_sem=S.snt)
    if o0 == 0:
        g.remote_dma_fused([copy(block(1 - h, m, q), [here], 0x0F00, S.arr)], local_sem=S.snt)
    sent += 16

    if k == COLLECTOR:
        g.wait_ge(S.msum, 8)
        g.remote_dma_fused([RemoteDMATransfer(dst_ids=[to(at(i % 2, i // 2, q, RANK)) for i in range(16)],
                                              dma_engine_mask=OFF_CHIP, remote_sem=S.sarr,
                                              srcs=[slab(T.cd, i) for i in range(17)],
                                              dsts=[slab(T.sd, me) for i in range(16)], alu_op=1)], local_sem=S.snt)
        sent += 8

    g.wait_ge(S.snt, sent)
